import numpy as np
import ml_dtypes


def mxq(x, axis, fmt="e4m3"):
    dtype, down = {"e4m3": (ml_dtypes.float8_e4m3fn, 7), "e5m2": (ml_dtypes.float8_e5m2, 14)}[fmt]
    v = np.moveaxis(np.asarray(x, np.float32).astype(ml_dtypes.bfloat16).astype(np.float64), axis, -1)
    blocks = v.reshape(v.shape[:-1] + (-1, 32))
    amax = np.abs(blocks).max(-1, keepdims=True)
    byte = np.maximum(np.where(amax > 0, np.frexp(amax)[1] - 1 + 127, 0) - down, 1)
    scale = np.exp2(byte - 127.0)
    codes = (blocks / scale).astype(np.float32).astype(dtype).astype(np.float64)
    return np.moveaxis((codes * scale).reshape(v.shape), -1, axis)


WIDE = False


def mx_kscale(k):
    if not WIDE:
        return np.ones(k)
    levels = np.array([10, -10, 5, -5, 0])
    if k % 512:
        return np.exp2(np.random.permutation(np.resize(levels, k // 32))).repeat(32)
    a = np.empty((k // 512, 16))
    for p in range(k // 512):
        a[p, :8] = np.random.permutation(np.resize(levels, 8))
        for g in range(8):
            far = levels[np.abs(levels - a[p, g]) >= 10]
            a[p, g + 8] = far[np.random.randint(len(far))]
    return np.exp2(a.ravel()).repeat(32)


def f64(x):
    return np.asarray(x).astype(np.float64)


def striped(idx):
    return np.tile(idx.reshape(-1, 16).T, (8, 1)).astype(np.uint16)


def unstriped(offs):
    return offs[:16].T.reshape(-1).astype(np.int64)


def pack_weight(w):
    k, n = w.shape
    w = f64(np.asarray(w, np.float32).astype(ml_dtypes.bfloat16)).reshape(k // 32, 32, n)
    amax = np.abs(w).max(1)
    byte = np.clip(np.where(amax > 0, np.frexp(amax)[1] - 1 + 127 - 7, 1), 1, 254)
    scaled = (w * np.exp2(127.0 - byte)[:, None, :]).reshape(k, n).astype(np.float32)
    words = np.ascontiguousarray(scaled.reshape(k // 512, 128, 4, n).transpose(0, 1, 3, 2)).astype(ml_dtypes.float8_e4m3fn).view(np.uint8)
    return words, np.ascontiguousarray(byte.astype(np.uint8).reshape(k // 512, 16, n))


def unpack_weight(words, scales):
    g, p, n, _ = words.shape
    vals = np.ascontiguousarray(words).view(ml_dtypes.float8_e4m3fn).astype(np.float64) * np.repeat(np.exp2(scales.astype(np.float64) - 127.0), 8, axis=1)[..., None]
    return vals.transpose(0, 1, 3, 2).reshape(g * 512, n)


def relu(v):
    return np.maximum(v, 0.0)


K, T, D, S, V, N = 1024, 2048, 4, 1024, 512, 128


def setup_inputs():
    n = np.random.standard_normal
    s = mx_kscale(K)[:, None]
    packed = pack_weight(n((K, T)) * s)
    return {
        "x_words": packed[0],
        "x_scales": packed[1],
        "w": (n((K, N)) / np.sqrt(K) / s).astype(np.float32),
        "b": (0.3 * n((N, 1))).astype(np.float32),
        "gate": np.tile(np.random.uniform(0.2, 1.0, (D, 1, V)) / np.sqrt(D), (1, N, 1)).astype(np.float32),
        "offs": striped(np.random.permutation(T)[:S]),
        "pos1": striped(np.random.permutation(S)[:V]),
        "pos2": striped(np.random.permutation(S)[:V]),
        "pos3": striped(np.random.permutation(S)[:V]),
        "pos4": striped(np.random.permutation(S)[:V]),
    }


def reference(x_words, x_scales, w, b, gate, offs, pos1, pos2, pos3, pos4):
    idx = unstriped(offs)
    xq = unpack_weight(x_words, x_scales)[:, idx]
    y = mxq(f64(w), 0, "e4m3").T @ xq
    y = relu(y + f64(b))
    return sum(f64(gate[d]) * y[:, unstriped(p)] for d, p in enumerate((pos1, pos2, pos3, pos4)))

@@ -1,0 +1,161 @@
+from contextlib import ExitStack
+
+import concourse.mybir as mybir
+from concourse.masks import make_identity
+
+K, T, D, S, V, N = 1024, 2048, 4, 1024, 512, 128
+FLOPS = 2 * K * N * S
+
+F32 = mybir.dt.float32
+BF16 = mybir.dt.bfloat16
+I32 = mybir.dt.int32
+U32 = mybir.dt.uint32
+U16 = mybir.dt.uint16
+U8 = mybir.dt.uint8
+FP8X4 = mybir.dt.float8_e4m3fn_x4
+ACT = mybir.ActivationFunctionType
+ALU = mybir.AluOpType
+
+P = 128
+PACK = 4
+PASSES = K // (P * PACK)
+STRIPE = 16
+PIECE = 256
+HALF = V // 2
+
+
+def tile_picked_sub_lin_relu_sub_p_kernel(
+    tc, x_words, x_scales, w, b, gate, offs, pos1, pos2, pos3, pos4, out
+):
+    nc = tc.nc
+    with ExitStack() as ctx:
+        keep = ctx.enter_context(tc.tile_pool(name="keep", bufs=1))
+        banks = ctx.enter_context(tc.psum_pool(name="banks", bufs=4))
+        sums = ctx.enter_context(tc.psum_pool(name="sums", bufs=2))
+
+        scale_table = keep.tile([P, T], U8, align_bytes=64)
+        nc.vector.memset(scale_table[:].bitcast(I32), 0)
+        identity = keep.tile([P, P], F32, align_bytes=64)
+        make_identity(nc, identity[:])
+
+        picks = keep.tile([P, S // STRIPE], U16)
+        nc.sync.dma_start(picks[:], offs)
+
+        w_raw = [keep.tile([P, PACK, N], F32, name=f"w_raw{o}") for o in range(PASSES)]
+        word_table = [keep.tile([P, T], U32, name=f"word_table{o}", align_bytes=64) for o in range(PASSES)]
+
+        def load_w(o):
+            rows = w[o * P * PACK : (o + 1) * P * PACK, :]
+            nc.sync.dma_start(w_raw[o][:], rows.rearrange("(p j) m -> p j m", j=PACK))
+
+        def load_words(o):
+            nc.sync.dma_start(word_table[o][:].bitcast(I32), x_words[o].rearrange("p c r -> p (c r)").bitcast(I32))
+
+        load_w(0)
+        for q in range(4):
+            nc.sync.dma_start(
+                scale_table[32 * q : 32 * q + 4 * PASSES, :].bitcast(I32),
+                x_scales[:, 4 * q : 4 * q + 4, :].bitcast(I32),
+            )
+        load_words(0)
+        load_w(1)
+        load_words(1)
+        bias = keep.tile([P, 1], F32)
+        nc.sync.dma_start(bias[:], b)
+        places = []
+        for d, pos in enumerate((pos1, pos2, pos3, pos4)):
+            place = keep.tile([P, V // STRIPE], U16, name=f"places{d}")
+            nc.sync.dma_start(place[:], pos)
+            places.append(place)
+        gates = []
+        for h in range(2):
+            gate_half = keep.tile([P, D, HALF], F32, name=f"gates{h}")
+            nc.sync.dma_start(gate_half[:], gate[:, :, h * HALF : (h + 1) * HALF].rearrange("d m v -> m d v"))
+            gates.append(gate_half)
+
+        w_grouped = [keep.tile([P, N, PACK], BF16, name=f"w_grouped{o}", align_bytes=64) for o in range(PASSES)]
+        for o in range(PASSES):
+            nc.scalar.activation(w_grouped[o][:], w_raw[o][:].rearrange("p j m -> p m j"), ACT.Copy)
+
+        picked_scales = keep.tile([P, S], U8, align_bytes=64)
+        nc.vector.tensor_copy(picked_scales[:], scale_table[:].indirect(picks[:]))
+        picked0 = keep.tile([P, S], U32, align_bytes=64)
+        nc.vector.tensor_copy(picked0[:], word_table[0][:].indirect(picks[:]))
+
+        w_codes = [keep.tile([P, N], U32, name=f"w_codes{o}", align_bytes=64) for o in range(PASSES)]
+        w_scales = [keep.tile([P, N], U8, name=f"w_scales{o}", align_bytes=64) for o in range(PASSES)]
+        for o in range(PASSES):
+            nc.vector.quantize_mx(
+                out=w_codes[o][:].bitcast(FP8X4),
+                scales=w_scales[o][:],
+                in_=w_grouped[o][:].rearrange("p m j -> p (m j)"),
+            )
+
+        y = keep.tile([P, S], F32, align_bytes=64)
+        pieces = [slice(i * PIECE, (i + 1) * PIECE) for i in range(S // PIECE)]
+        acc = [banks.tile([P, PIECE], F32, tag="bank", name=f"acc{i}") for i in range(len(pieces))]
+        for i, cols in enumerate(pieces):
+            nc.tensor.matmul_mx(
+                out=acc[i][:],
+                lhsT=w_codes[0][:].bitcast(FP8X4),
+                lhsT_scale=w_scales[0][:],
+                rhs=picked0[:, cols].bitcast(FP8X4),
+                rhs_scale=picked_scales[:, cols],
+                start=True,
+                stop=False,
+            )
+        for i, cols in enumerate(pieces):
+            picked1 = keep.tile([P, PIECE], U32, name=f"picked1_{i}", align_bytes=64)
+            nc.vector.tensor_copy(
+                picked1[:], word_table[1][:].indirect(picks[:, cols.start // STRIPE : cols.stop // STRIPE])
+            )
+            nc.tensor.matmul_mx(
+                out=acc[i][:],
+                lhsT=w_codes[1][:].bitcast(FP8X4),
+                lhsT_scale=w_scales[1][:],
+                rhs=picked1[:].bitcast(FP8X4),
+                rhs_scale=picked_scales[4:P, cols],
+                start=False,
+                stop=True,
+            )
+            nc.scalar.activation(y[:, cols], acc[i][:], ACT.Relu, bias=bias[:])
+
+        def weighted(h, d):
+            term = keep.tile([P, HALF], F32, name=f"term{h}_{d}", align_bytes=64)
+            entries = places[d][:, h * HALF // STRIPE : (h + 1) * HALF // STRIPE]
+            nc.vector.tensor_tensor(term[:], y[:].indirect(entries), gates[h][:, d, :], ALU.mult)
+            return term
+
+        def summed_on_tensor(h, count):
+            turned = [banks.tile([P, P], F32, tag="bank", name=f"turned{h}_{c}") for c in range(HALF // P)]
+            for d in range(count):
+                term = weighted(h, d)
+                for c in range(HALF // P):
+                    nc.tensor.matmul(
+                        turned[c][:],
+                        lhsT=term[:, c * P : (c + 1) * P],
+                        rhs=identity[:],
+                        is_transpose=True,
+                        start=(d == 0),
+                        stop=(d == count - 1),
+                    )
+            total = sums.tile([P, HALF], F32, tag="sum", name=f"total{h}")
+            for c in range(HALF // P):
+                staged = keep.tile([P, P], F32, name=f"staged{h}_{c}", align_bytes=64)
+                nc.scalar.copy(staged[:], turned[c][:])
+                nc.tensor.transpose(total[:, c * P : (c + 1) * P], staged[:], identity[:])
+            return total
+
+        first = summed_on_tensor(0, D)
+        first_out = keep.tile([P, HALF], F32)
+        nc.scalar.copy(first_out[:], first[:])
+        nc.sync.dma_start(out[:, 0:HALF], first_out[:])
+
+        early = summed_on_tensor(1, 2)
+        third = weighted(1, 2)
+        fourth = weighted(1, 3)
+        late = keep.tile([P, HALF], F32)
+        nc.vector.tensor_tensor(late[:], third[:], fourth[:], ALU.add)
+        second_out = keep.tile([P, HALF], F32)
+        nc.vector.tensor_tensor(second_out[:], late[:], early[:], ALU.add)
+        nc.sync.dma_start(out[:, HALF:V], second_out[:])

@@ -22,6 +22,8 @@ PASSES = K // (P * PACK)
 STRIPE = 16
 PIECE = 256
 HALF = V // 2
+SCALE_ROWS = 16
+SCALE_ROW0 = P - PASSES * SCALE_ROWS
 
 
 def tile_picked_sub_lin_relu_sub_p_kernel(
@@ -30,11 +32,17 @@ def tile_picked_sub_lin_relu_sub_p_kernel(
     nc = tc.nc
     with ExitStack() as ctx:
         keep = ctx.enter_context(tc.tile_pool(name="keep", bufs=1))
-        banks = ctx.enter_context(tc.psum_pool(name="banks", bufs=4))
+        banks = ctx.enter_context(tc.psum_pool(name="banks", bufs=5))
         sums = ctx.enter_context(tc.psum_pool(name="sums", bufs=2))
 
+        warm = keep.tile([P, 2], F32)
+        nc.vector.memset(warm[:, 0:1], 0.0)
+        nc.scalar.activation(warm[:, 1:2], warm[:, 0:1], ACT.Relu)
+
         scale_table = keep.tile([P, T], U8, align_bytes=64)
-        nc.vector.memset(scale_table[:].bitcast(I32), 0)
+        nc.vector.memset(scale_table[0:SCALE_ROW0, :].bitcast(I32), 0)
+        planes = keep.tile([P, S], U8, align_bytes=64)
+        nc.vector.memset(planes[:].bitcast(I32), 0)
         identity = keep.tile([P, P], F32, align_bytes=64)
         make_identity(nc, identity[:])
 
@@ -42,7 +50,9 @@ def tile_picked_sub_lin_relu_sub_p_kernel(
         nc.sync.dma_start(picks[:], offs)
 
         w_raw = [keep.tile([P, PACK, N], F32, name=f"w_raw{o}") for o in range(PASSES)]
-        word_table = [keep.tile([P, T], U32, name=f"word_table{o}", align_bytes=64) for o in range(PASSES)]
+        word_table = [
+            keep.tile([P, T], U32, name=f"word_table{o}", tag=f"table{o}", align_bytes=64) for o in range(PASSES)
+        ]
 
         def load_w(o):
             rows = w[o * P * PACK : (o + 1) * P * PACK, :]
@@ -51,13 +61,14 @@ def tile_picked_sub_lin_relu_sub_p_kernel(
         def load_words(o):
             nc.sync.dma_start(word_table[o][:].bitcast(I32), x_words[o].rearrange("p c r -> p (c r)").bitcast(I32))
 
-        load_w(0)
-        for q in range(4):
+        for o in range(PASSES):
+            row = SCALE_ROW0 + SCALE_ROWS * o
             nc.sync.dma_start(
-                scale_table[32 * q : 32 * q + 4 * PASSES, :].bitcast(I32),
-                x_scales[:, 4 * q : 4 * q + 4, :].bitcast(I32),
+                scale_table[row : row + SCALE_ROWS, :].bitcast(I32),
+                x_scales[o].rearrange("(q r) c -> r q c", r=4).bitcast(I32),
             )
         load_words(0)
+        load_w(0)
         load_w(1)
         load_words(1)
         bias = keep.tile([P, 1], F32)
@@ -67,20 +78,27 @@ def tile_picked_sub_lin_relu_sub_p_kernel(
             place = keep.tile([P, V // STRIPE], U16, name=f"places{d}")
             nc.sync.dma_start(place[:], pos)
             places.append(place)
-        gates = []
-        for h in range(2):
-            gate_half = keep.tile([P, D, HALF], F32, name=f"gates{h}")
-            nc.sync.dma_start(gate_half[:], gate[:, :, h * HALF : (h + 1) * HALF].rearrange("d m v -> m d v"))
-            gates.append(gate_half)
-
-        w_grouped = [keep.tile([P, N, PACK], BF16, name=f"w_grouped{o}", align_bytes=64) for o in range(PASSES)]
-        for o in range(PASSES):
-            nc.scalar.activation(w_grouped[o][:], w_raw[o][:].rearrange("p j m -> p m j"), ACT.Copy)
 
         picked_scales = keep.tile([P, S], U8, align_bytes=64)
         nc.vector.tensor_copy(picked_scales[:], scale_table[:].indirect(picks[:]))
+        for q in range(4):
+            nc.scalar.dma_start(
+                planes[32 * q : 32 * q + 4 * PASSES, :].bitcast(I32),
+                picked_scales[SCALE_ROW0 + q : P : 4, :].bitcast(I32),
+            )
         picked0 = keep.tile([P, S], U32, align_bytes=64)
         nc.vector.tensor_copy(picked0[:], word_table[0][:].indirect(picks[:]))
+
+        gates = keep.tile([P, D * V], F32, tag="table0", align_bytes=64)
+        for d in range(0, D, 2):
+            nc.sync.dma_start(
+                gates[:, d * V : (d + 2) * V].rearrange("m (d v) -> m d v", v=V),
+                gate[d : d + 2].rearrange("d m v -> m d v"),
+            )
+
+        w_grouped = [keep.tile([P, N, PACK], BF16, name=f"w_grouped{o}", align_bytes=64) for o in range(PASSES)]
+        for o in range(PASSES):
+            nc.scalar.copy(w_grouped[o][:], w_raw[o][:].rearrange("p j m -> p m j"))
 
         w_codes = [keep.tile([P, N], U32, name=f"w_codes{o}", align_bytes=64) for o in range(PASSES)]
         w_scales = [keep.tile([P, N], U8, name=f"w_scales{o}", align_bytes=64) for o in range(PASSES)]
@@ -93,69 +111,72 @@ def tile_picked_sub_lin_relu_sub_p_kernel(
 
         y = keep.tile([P, S], F32, align_bytes=64)
         pieces = [slice(i * PIECE, (i + 1) * PIECE) for i in range(S // PIECE)]
-        acc = [banks.tile([P, PIECE], F32, tag="bank", name=f"acc{i}") for i in range(len(pieces))]
-        for i, cols in enumerate(pieces):
+        groups = pieces[:-1] + [slice(S - PIECE, S - P), slice(S - P, S)]
+        acc = [banks.tile([P, g.stop - g.start], F32, tag="bank", name=f"acc{g.start}") for g in groups]
+        for bank, cols in zip(acc, groups):
             nc.tensor.matmul_mx(
-                out=acc[i][:],
+                out=bank[:],
                 lhsT=w_codes[0][:].bitcast(FP8X4),
                 lhsT_scale=w_scales[0][:],
                 rhs=picked0[:, cols].bitcast(FP8X4),
-                rhs_scale=picked_scales[:, cols],
+                rhs_scale=planes[:, cols],
                 start=True,
                 stop=False,
             )
-        for i, cols in enumerate(pieces):
-            picked1 = keep.tile([P, PIECE], U32, name=f"picked1_{i}", align_bytes=64)
+        picked1 = keep.tile([P, S], U32, align_bytes=64)
+        for cols in pieces:
             nc.vector.tensor_copy(
-                picked1[:], word_table[1][:].indirect(picks[:, cols.start // STRIPE : cols.stop // STRIPE])
+                picked1[:, cols], word_table[1][:].indirect(picks[:, cols.start // STRIPE : cols.stop // STRIPE])
             )
+        for bank, cols in zip(acc, groups):
             nc.tensor.matmul_mx(
-                out=acc[i][:],
+                out=bank[:],
                 lhsT=w_codes[1][:].bitcast(FP8X4),
                 lhsT_scale=w_scales[1][:],
-                rhs=picked1[:].bitcast(FP8X4),
-                rhs_scale=picked_scales[4:P, cols],
+                rhs=picked1[:, cols].bitcast(FP8X4),
+                rhs_scale=planes[4:P, cols],
                 start=False,
                 stop=True,
             )
-            nc.scalar.activation(y[:, cols], acc[i][:], ACT.Relu, bias=bias[:])
+            nc.scalar.activation(y[:, cols], bank[:], ACT.Relu, bias=bias[:])
 
-        def weighted(h, d):
-            term = keep.tile([P, HALF], F32, name=f"term{h}_{d}", align_bytes=64)
-            entries = places[d][:, h * HALF // STRIPE : (h + 1) * HALF // STRIPE]
-            nc.vector.tensor_tensor(term[:], y[:].indirect(entries), gates[h][:, d, :], ALU.mult)
-            return term
+        terms = [keep.tile([P, V], F32, name=f"term{d}", align_bytes=64) for d in range(D)]
 
-        def summed_on_tensor(h, count):
-            turned = [banks.tile([P, P], F32, tag="bank", name=f"turned{h}_{c}") for c in range(HALF // P)]
-            for d in range(count):
-                term = weighted(h, d)
-                for c in range(HALF // P):
-                    nc.tensor.matmul(
-                        turned[c][:],
-                        lhsT=term[:, c * P : (c + 1) * P],
-                        rhs=identity[:],
-                        is_transpose=True,
-                        start=(d == 0),
-                        stop=(d == count - 1),
-                    )
-            total = sums.tile([P, HALF], F32, tag="sum", name=f"total{h}")
-            for c in range(HALF // P):
-                staged = keep.tile([P, P], F32, name=f"staged{h}_{c}", align_bytes=64)
+        def weighted(d, cols):
+            entries = places[d][:, cols.start // STRIPE : cols.stop // STRIPE]
+            weights = gates[:, d * V + cols.start : d * V + cols.stop]
+            nc.vector.tensor_tensor(terms[d][:, cols], y[:].indirect(entries), weights, ALU.mult)
+
+        halves = [slice(0, HALF), slice(HALF, V)]
+        blocks = [slice(c * P, (c + 1) * P) for c in range(V // P)]
+        turned = [banks.tile([P, P], F32, tag="bank", name=f"turned{c}") for c in range(len(blocks))]
+        totals = [sums.tile([P, HALF], F32, tag="sum", name=f"total{h}") for h in range(len(halves))]
+
+        def add_turned(d, cols):
+            for c in range(cols.start // P, cols.stop // P):
+                nc.tensor.matmul(
+                    turned[c][:],
+                    lhsT=terms[d][:, blocks[c]],
+                    rhs=identity[:],
+                    is_transpose=True,
+                    start=(d == 0),
+                    stop=(d == D - 2),
+                )
+
+        for d in range(D - 2):
+            weighted(d, slice(0, V))
+            add_turned(d, slice(0, V))
+        for cols in [halves[0]] + blocks[HALF // P :]:
+            weighted(D - 2, cols)
+            add_turned(D - 2, cols)
+            for c in range(cols.start // P, cols.stop // P):
+                staged = keep.tile([P, P], F32, name=f"staged{c}", align_bytes=64)
                 nc.scalar.copy(staged[:], turned[c][:])
-                nc.tensor.transpose(total[:, c * P : (c + 1) * P], staged[:], identity[:])
-            return total
-
-        first = summed_on_tensor(0, D)
-        first_out = keep.tile([P, HALF], F32)
-        nc.scalar.copy(first_out[:], first[:])
-        nc.sync.dma_start(out[:, 0:HALF], first_out[:])
-
-        early = summed_on_tensor(1, 2)
-        third = weighted(1, 2)
-        fourth = weighted(1, 3)
-        late = keep.tile([P, HALF], F32)
-        nc.vector.tensor_tensor(late[:], third[:], fourth[:], ALU.add)
-        second_out = keep.tile([P, HALF], F32)
-        nc.vector.tensor_tensor(second_out[:], late[:], early[:], ALU.add)
-        nc.sync.dma_start(out[:, HALF:V], second_out[:])
+                h, offset = divmod(c * P, HALF)
+                nc.tensor.transpose(totals[h][:, offset : offset + P], staged[:], identity[:])
+        for cols in halves:
+            weighted(D - 1, cols)
+        for total, cols in zip(totals, halves):
+            result = keep.tile([P, HALF], F32, name=f"result{cols.start}")
+            nc.vector.tensor_tensor(result[:], terms[D - 1][:, cols], total[:], ALU.add)
+            nc.sync.dma_start(out[:, cols], result[:])

@@ -46,9 +46,6 @@ def tile_picked_sub_lin_relu_sub_p_kernel(
         identity = keep.tile([P, P], F32, align_bytes=64)
         make_identity(nc, identity[:])
 
-        picks = keep.tile([P, S // STRIPE], U16)
-        nc.sync.dma_start(picks[:], offs)
-
         w_raw = [keep.tile([P, PACK, N], F32, name=f"w_raw{o}") for o in range(PASSES)]
         word_table = [
             keep.tile([P, T], U32, name=f"word_table{o}", tag=f"table{o}", align_bytes=64) for o in range(PASSES)
@@ -67,10 +64,12 @@ def tile_picked_sub_lin_relu_sub_p_kernel(
                 scale_table[row : row + SCALE_ROWS, :].bitcast(I32),
                 x_scales[o].rearrange("(q r) c -> r q c", r=4).bitcast(I32),
             )
+        picks = keep.tile([P, S // STRIPE], U16)
+        nc.sync.dma_start(picks[:], offs)
         load_words(0)
         load_w(0)
-        load_w(1)
         load_words(1)
+        load_w(1)
         bias = keep.tile([P, 1], F32)
         nc.sync.dma_start(bias[:], b)
         places = []
@@ -96,19 +95,24 @@ def tile_picked_sub_lin_relu_sub_p_kernel(
                 gate[d : d + 2].rearrange("d m v -> m d v"),
             )
 
-        w_grouped = [keep.tile([P, N, PACK], BF16, name=f"w_grouped{o}", align_bytes=64) for o in range(PASSES)]
+        w_grouped = [
+            keep.tile([P, N, PACK], BF16, name=f"w_grouped{o}", tag=f"grouped{o}", align_bytes=64)
+            for o in range(PASSES)
+        ]
         for o in range(PASSES):
             nc.scalar.copy(w_grouped[o][:], w_raw[o][:].rearrange("p j m -> p m j"))
 
         w_codes = [keep.tile([P, N], U32, name=f"w_codes{o}", align_bytes=64) for o in range(PASSES)]
         w_scales = [keep.tile([P, N], U8, name=f"w_scales{o}", align_bytes=64) for o in range(PASSES)]
-        for o in range(PASSES):
+
+        def quantize_w(o):
             nc.vector.quantize_mx(
                 out=w_codes[o][:].bitcast(FP8X4),
                 scales=w_scales[o][:],
                 in_=w_grouped[o][:].rearrange("p m j -> p (m j)"),
             )
 
+        quantize_w(0)
         y = keep.tile([P, S], F32, align_bytes=64)
         pieces = [slice(i * PIECE, (i + 1) * PIECE) for i in range(S // PIECE)]
         groups = pieces[:-1] + [slice(S - PIECE, S - P), slice(S - P, S)]
@@ -123,22 +127,32 @@ def tile_picked_sub_lin_relu_sub_p_kernel(
                 start=True,
                 stop=False,
             )
-        picked1 = keep.tile([P, S], U32, align_bytes=64)
-        for cols in pieces:
+        picked1 = keep.tile([P, S - PIECE], U32, align_bytes=64)
+        for cols in pieces[:-1]:
             nc.vector.tensor_copy(
                 picked1[:, cols], word_table[1][:].indirect(picks[:, cols.start // STRIPE : cols.stop // STRIPE])
             )
-        for bank, cols in zip(acc, groups):
+        quantize_w(1)
+        picked_last = keep.tile([P, PIECE], U32, tag="grouped1", align_bytes=64)
+        nc.vector.tensor_copy(picked_last[:], word_table[1][:].indirect(picks[:, (S - PIECE) // STRIPE :]))
+        for i, (bank, cols) in enumerate(zip(acc, groups)):
+            if cols.stop <= S - PIECE:
+                words = picked1[:, cols]
+            else:
+                words = picked_last[:, cols.start - (S - PIECE) : cols.stop - (S - PIECE)]
             nc.tensor.matmul_mx(
                 out=bank[:],
                 lhsT=w_codes[1][:].bitcast(FP8X4),
                 lhsT_scale=w_scales[1][:],
-                rhs=picked1[:, cols].bitcast(FP8X4),
+                rhs=words.bitcast(FP8X4),
                 rhs_scale=planes[4:P, cols],
                 start=False,
                 stop=True,
             )
-            nc.scalar.activation(y[:, cols], bank[:], ACT.Relu, bias=bias[:])
+            if i % 2 == 0:
+                nc.scalar.activation(y[:, cols], bank[:], ACT.Relu, bias=bias[:])
+            else:
+                nc.vector.tensor_scalar(y[:, cols], bank[:], bias[:], 0.0, ALU.add, ALU.max)
 
         terms = [keep.tile([P, V], F32, name=f"term{d}", align_bytes=64) for d in range(D)]
 

from contextlib import ExitStack

import concourse.mybir as mybir
from concourse.masks import make_identity

K, T, D, S, V, N = 1024, 2048, 4, 1024, 512, 128
FLOPS = 2 * K * N * S

F32 = mybir.dt.float32
BF16 = mybir.dt.bfloat16
I32 = mybir.dt.int32
U32 = mybir.dt.uint32
U16 = mybir.dt.uint16
U8 = mybir.dt.uint8
FP8X4 = mybir.dt.float8_e4m3fn_x4
ACT = mybir.ActivationFunctionType
ALU = mybir.AluOpType

P = 128
PACK = 4
PASSES = K // (P * PACK)
STRIPE = 16
PIECE = 256
HALF = V // 2
SCALE_ROWS = 16
SCALE_ROW0 = P - PASSES * SCALE_ROWS


def tile_picked_sub_lin_relu_sub_p_kernel(
    tc, x_words, x_scales, w, b, gate, offs, pos1, pos2, pos3, pos4, out
):
    nc = tc.nc
    with ExitStack() as ctx:
        keep = ctx.enter_context(tc.tile_pool(name="keep", bufs=1))
        banks = ctx.enter_context(tc.psum_pool(name="banks", bufs=5))
        sums = ctx.enter_context(tc.psum_pool(name="sums", bufs=2))

        warm = keep.tile([P, 2], F32)
        nc.vector.memset(warm[:, 0:1], 0.0)
        nc.scalar.activation(warm[:, 1:2], warm[:, 0:1], ACT.Relu)

        scale_table = keep.tile([P, T], U8, align_bytes=64)
        nc.vector.memset(scale_table[0:SCALE_ROW0, :].bitcast(I32), 0)
        planes = keep.tile([P, S], U8, align_bytes=64)
        nc.vector.memset(planes[:].bitcast(I32), 0)
        identity = keep.tile([P, P], F32, align_bytes=64)
        make_identity(nc, identity[:])

        w_raw = [keep.tile([P, PACK, N], F32, name=f"w_raw{o}") for o in range(PASSES)]
        word_table = [
            keep.tile([P, T], U32, name=f"word_table{o}", tag=f"table{o}", align_bytes=64) for o in range(PASSES)
        ]

        def load_w(o):
            rows = w[o * P * PACK : (o + 1) * P * PACK, :]
            nc.sync.dma_start(w_raw[o][:], rows.rearrange("(p j) m -> p j m", j=PACK))

        def load_words(o):
            nc.sync.dma_start(word_table[o][:].bitcast(I32), x_words[o].rearrange("p c r -> p (c r)").bitcast(I32))

        for o in range(PASSES):
            row = SCALE_ROW0 + SCALE_ROWS * o
            nc.sync.dma_start(
                scale_table[row : row + SCALE_ROWS, :].bitcast(I32),
                x_scales[o].rearrange("(q r) c -> r q c", r=4).bitcast(I32),
            )
        picks = keep.tile([P, S // STRIPE], U16)
        nc.sync.dma_start(picks[:], offs)
        load_words(0)
        load_w(0)
        load_words(1)
        load_w(1)
        bias = keep.tile([P, 1], F32)
        nc.sync.dma_start(bias[:], b)
        places = []
        for d, pos in enumerate((pos1, pos2, pos3, pos4)):
            place = keep.tile([P, V // STRIPE], U16, name=f"places{d}")
            nc.sync.dma_start(place[:], pos)
            places.append(place)

        picked_scales = keep.tile([P, S], U8, align_bytes=64)
        nc.vector.tensor_copy(picked_scales[:], scale_table[:].indirect(picks[:]))
        for q in range(4):
            nc.scalar.dma_start(
                planes[32 * q : 32 * q + 4 * PASSES, :].bitcast(I32),
                picked_scales[SCALE_ROW0 + q : P : 4, :].bitcast(I32),
            )
        picked0 = keep.tile([P, S], U32, align_bytes=64)
        nc.vector.tensor_copy(picked0[:], word_table[0][:].indirect(picks[:]))

        gates = keep.tile([P, D * V], F32, tag="table0", align_bytes=64)
        for d in range(0, D, 2):
            nc.sync.dma_start(
                gates[:, d * V : (d + 2) * V].rearrange("m (d v) -> m d v", v=V),
                gate[d : d + 2].rearrange("d m v -> m d v"),
            )

        w_grouped = [
            keep.tile([P, N, PACK], BF16, name=f"w_grouped{o}", tag=f"grouped{o}", align_bytes=64)
            for o in range(PASSES)
        ]
        for o in range(PASSES):
            nc.scalar.copy(w_grouped[o][:], w_raw[o][:].rearrange("p j m -> p m j"))

        w_codes = [keep.tile([P, N], U32, name=f"w_codes{o}", align_bytes=64) for o in range(PASSES)]
        w_scales = [keep.tile([P, N], U8, name=f"w_scales{o}", align_bytes=64) for o in range(PASSES)]

        def quantize_w(o):
            nc.vector.quantize_mx(
                out=w_codes[o][:].bitcast(FP8X4),
                scales=w_scales[o][:],
                in_=w_grouped[o][:].rearrange("p m j -> p (m j)"),
            )

        quantize_w(0)
        y = keep.tile([P, S], F32, align_bytes=64)
        pieces = [slice(i * PIECE, (i + 1) * PIECE) for i in range(S // PIECE)]
        groups = pieces[:-1] + [slice(S - PIECE, S - P), slice(S - P, S)]
        acc = [banks.tile([P, g.stop - g.start], F32, tag="bank", name=f"acc{g.start}") for g in groups]
        for bank, cols in zip(acc, groups):
            nc.tensor.matmul_mx(
                out=bank[:],
                lhsT=w_codes[0][:].bitcast(FP8X4),
                lhsT_scale=w_scales[0][:],
                rhs=picked0[:, cols].bitcast(FP8X4),
                rhs_scale=planes[:, cols],
                start=True,
                stop=False,
            )
        picked1 = keep.tile([P, S - PIECE], U32, align_bytes=64)
        for cols in pieces[:-1]:
            nc.vector.tensor_copy(
                picked1[:, cols], word_table[1][:].indirect(picks[:, cols.start // STRIPE : cols.stop // STRIPE])
            )
        quantize_w(1)
        picked_last = keep.tile([P, PIECE], U32, tag="grouped1", align_bytes=64)
        nc.vector.tensor_copy(picked_last[:], word_table[1][:].indirect(picks[:, (S - PIECE) // STRIPE :]))
        for i, (bank, cols) in enumerate(zip(acc, groups)):
            if cols.stop <= S - PIECE:
                words = picked1[:, cols]
            else:
                words = picked_last[:, cols.start - (S - PIECE) : cols.stop - (S - PIECE)]
            nc.tensor.matmul_mx(
                out=bank[:],
                lhsT=w_codes[1][:].bitcast(FP8X4),
                lhsT_scale=w_scales[1][:],
                rhs=words.bitcast(FP8X4),
                rhs_scale=planes[4:P, cols],
                start=False,
                stop=True,
            )
            if i % 2 == 0:
                nc.scalar.activation(y[:, cols], bank[:], ACT.Relu, bias=bias[:])
            else:
                nc.vector.tensor_scalar(y[:, cols], bank[:], bias[:], 0.0, ALU.add, ALU.max)

        terms = [keep.tile([P, V], F32, name=f"term{d}", align_bytes=64) for d in range(D)]

        def weighted(d, cols):
            entries = places[d][:, cols.start // STRIPE : cols.stop // STRIPE]
            weights = gates[:, d * V + cols.start : d * V + cols.stop]
            nc.vector.tensor_tensor(terms[d][:, cols], y[:].indirect(entries), weights, ALU.mult)

        halves = [slice(0, HALF), slice(HALF, V)]
        blocks = [slice(c * P, (c + 1) * P) for c in range(V // P)]
        turned = [banks.tile([P, P], F32, tag="bank", name=f"turned{c}") for c in range(len(blocks))]
        totals = [sums.tile([P, HALF], F32, tag="sum", name=f"total{h}") for h in range(len(halves))]

        def add_turned(d, cols):
            for c in range(cols.start // P, cols.stop // P):
                nc.tensor.matmul(
                    turned[c][:],
                    lhsT=terms[d][:, blocks[c]],
                    rhs=identity[:],
                    is_transpose=True,
                    start=(d == 0),
                    stop=(d == D - 2),
                )

        for d in range(D - 2):
            weighted(d, slice(0, V))
            add_turned(d, slice(0, V))
        for cols in [halves[0]] + blocks[HALF // P :]:
            weighted(D - 2, cols)
            add_turned(D - 2, cols)
            for c in range(cols.start // P, cols.stop // P):
                staged = keep.tile([P, P], F32, name=f"staged{c}", align_bytes=64)
                nc.scalar.copy(staged[:], turned[c][:])
                h, offset = divmod(c * P, HALF)
                nc.tensor.transpose(totals[h][:, offset : offset + P], staged[:], identity[:])
        for cols in halves:
            weighted(D - 1, cols)
        for total, cols in zip(totals, halves):
            result = keep.tile([P, HALF], F32, name=f"result{cols.start}")
            nc.vector.tensor_tensor(result[:], terms[D - 1][:, cols], total[:], ALU.add)
            nc.sync.dma_start(out[:, cols], result[:])
